import numpy as np
import ml_dtypes


def mxq(x, axis, fmt="e4m3"):
    dtype, down = {"e4m3": (ml_dtypes.float8_e4m3fn, 7), "e5m2": (ml_dtypes.float8_e5m2, 14)}[fmt]
    v = np.moveaxis(np.asarray(x, np.float32).astype(ml_dtypes.bfloat16).astype(np.float64), axis, -1)
    blocks = v.reshape(v.shape[:-1] + (-1, 32))
    amax = np.abs(blocks).max(-1, keepdims=True)
    byte = np.maximum(np.where(amax > 0, np.frexp(amax)[1] - 1 + 127, 0) - down, 1)
    scale = np.exp2(byte - 127.0)
    codes = (blocks / scale).astype(np.float32).astype(dtype).astype(np.float64)
    return np.moveaxis((codes * scale).reshape(v.shape), -1, axis)


WIDE = False


def mx_kscale(k):
    if not WIDE:
        return np.ones(k)
    levels = np.array([10, -10, 5, -5, 0])
    if k % 512:
        return np.exp2(np.random.permutation(np.resize(levels, k // 32))).repeat(32)
    a = np.empty((k // 512, 16))
    for p in range(k // 512):
        a[p, :8] = np.random.permutation(np.resize(levels, 8))
        for g in range(8):
            far = levels[np.abs(levels - a[p, g]) >= 10]
            a[p, g + 8] = far[np.random.randint(len(far))]
    return np.exp2(a.ravel()).repeat(32)


def f64(x):
    return np.asarray(x).astype(np.float64)


def striped(idx):
    return np.tile(idx.reshape(-1, 16).T, (8, 1)).astype(np.uint16)


def unstriped(offs):
    return offs[:16].T.reshape(-1).astype(np.int64)


def pack_weight(w):
    k, n = w.shape
    w = f64(np.asarray(w, np.float32).astype(ml_dtypes.bfloat16)).reshape(k // 32, 32, n)
    amax = np.abs(w).max(1)
    byte = np.clip(np.where(amax > 0, np.frexp(amax)[1] - 1 + 127 - 7, 1), 1, 254)
    scaled = (w * np.exp2(127.0 - byte)[:, None, :]).reshape(k, n).astype(np.float32)
    words = np.ascontiguousarray(scaled.reshape(k // 512, 128, 4, n).transpose(0, 1, 3, 2)).astype(ml_dtypes.float8_e4m3fn).view(np.uint8)
    return words, np.ascontiguousarray(byte.astype(np.uint8).reshape(k // 512, 16, n))


def unpack_weight(words, scales):
    g, p, n, _ = words.shape
    vals = np.ascontiguousarray(words).view(ml_dtypes.float8_e4m3fn).astype(np.float64) * np.repeat(np.exp2(scales.astype(np.float64) - 127.0), 8, axis=1)[..., None]
    return vals.transpose(0, 1, 3, 2).reshape(g * 512, n)


def sigmoid(v):
    return 1.0 / (1.0 + np.exp(-np.maximum(v, -700.0)))


K, T, S, D, N, V = 512, 1024, 512, 4, 256, 128
P = 2 ** 7


def setup_inputs():
    n = np.random.standard_normal
    s = mx_kscale(K)[:, None]
    packed_xT = pack_weight(n((K, T)) * s)
    return {
        "x_words": packed_xT[0],
        "x_scales": packed_xT[1],
        "w1": (n((K, N)) / np.sqrt(K) / s).astype(np.float32),
        "w2": (n((K, N)) / np.sqrt(K) / s).astype(np.float32),
        "px": (n((N, V))).astype(np.float32),
        "py": (n((N, V))).astype(np.float32),
        "bx": (np.tile(n(S), (P, 1))).astype(np.float32),
        "by": (np.tile(n(S), (P, 1))).astype(np.float32),
        "il": (np.tile(np.random.uniform(0.5, 1.5, S), (P, 1))).astype(np.float32),
        "crit": (-np.random.uniform(1.0, 2.5, (N, 1))).astype(np.float32),
        "offs": striped(np.random.permutation(T)[:S]),
    }


def reference(x_words, x_scales, w1, w2, px, py, bx, by, il, crit, offs):
    xq = unpack_weight(x_words, x_scales)[:, unstriped(offs)]
    y = mxq(f64(w1), 0, "e4m3").T @ xq
    dx = y - (np.repeat(f64(px), D, axis=1)) + f64(bx)[:1]
    z = mxq(f64(w2), 0, "e4m3").T @ xq
    dy = z - (np.repeat(f64(py), D, axis=1)) + f64(by)[:1]
    ln = np.sqrt((dx) ** 2 + (dy) ** 2 + 0.05)
    stc = ln * f64(il)[:1]
    mu = sigmoid(-4.0 * (stc + f64(crit)))
    fb = (((stc - 1.0) * mu) * dx) / ln
    return fb.reshape(len(fb), -1, D).sum(axis=2)

@@ -1,0 +1,191 @@
+from contextlib import ExitStack
+
+import concourse.mybir as mybir
+from concourse.masks import make_identity
+
+K, T, S, D, N, V = 512, 1024, 512, 4, 256, 128
+P = 128
+PACK = 4
+HALVES = N // P
+SPLIT = 144
+FLOPS = 2 * 2 * K * N * S
+
+F32 = mybir.dt.float32
+BF16 = mybir.dt.bfloat16
+I32 = mybir.dt.int32
+U32 = mybir.dt.uint32
+U16 = mybir.dt.uint16
+U8 = mybir.dt.uint8
+FP8X4 = mybir.dt.float8_e4m3fn_x4
+ALU = mybir.AluOpType
+ACT = mybir.ActivationFunctionType
+
+
+def tile_picked_yperid_force_p_kernel(
+    tc, x_words, x_scales, w1, w2, px, py, bx, by, il, crit, offs, out
+):
+    nc = tc.nc
+    with ExitStack() as ctx:
+        sb = ctx.enter_context(tc.tile_pool(name="sb", bufs=1))
+        ps = ctx.enter_context(tc.psum_pool(name="ps", bufs=1))
+
+        offsets = sb.tile([P, S // 16], U16, name="offsets")
+        nc.sync.dma_start(offsets[:], offs)
+
+        scale_table = sb.tile([P, T], U8, name="scale_table", align_bytes=64)
+        nc.vector.memset(scale_table[:].bitcast(I32), 0)
+        for q in range(4):
+            nc.scalar.dma_start(
+                scale_table[32 * q : 32 * q + 4, :].bitcast(I32),
+                x_scales[0, 4 * q : 4 * q + 4, :].bitcast(I32),
+            )
+        word_table = sb.tile([P, T], I32, name="word_table", align_bytes=64)
+        nc.sync.dma_start(word_table[:], x_words[0].rearrange("p n t -> p (n t)").bitcast(I32))
+
+        w_raw = []
+        for c, w in enumerate((w1, w2)):
+            raw = sb.tile([P, PACK, N], F32, name="w_raw%d" % c)
+            nc.sync.dma_start(raw[:], w.rearrange("(p t) n -> p t n", t=PACK))
+            w_raw.append(raw)
+
+        ident = sb.tile([P, P], F32, name="ident")
+        make_identity(nc, ident[:])
+        one = sb.tile([P, 1], F32, name="one")
+        nc.gpsimd.memset(one[:], 1.0)
+        warm = sb.tile([P, 1], F32, name="warm")
+        nc.scalar.activation(warm[:], one[:], ACT.Abs_reciprocal_sqrt)
+
+        point = []
+        for c, pt in enumerate((px, py)):
+            t = sb.tile([P, HALVES, V], F32, name="point%d" % c)
+            nc.scalar.dma_start(t[:], pt.rearrange("(h p) v -> p h v", p=P))
+            point.append(t)
+        cols = []
+        for c, row in enumerate((bx, by, il)):
+            t = sb.tile([P, D], F32, name="col%d" % c)
+            nc.sync.dma_start(t[:], row[0:1, :].rearrange("o (v d) -> (o v) d", d=D))
+            cols.append(t)
+        bond = cols[:2]
+        inv_len = cols[2]
+        crit_col = sb.tile([P, HALVES, 1], F32, name="crit_col")
+        with nc.allow_non_contiguous_dma(reason="one value a partition"):
+            nc.sync.dma_start(crit_col[:], crit.rearrange("(h p) o -> p h o", p=P))
+
+
+        scale_picked = sb.tile([P, S], U8, name="scale_picked", align_bytes=64)
+        nc.vector.tensor_copy(scale_picked[:], scale_table[:].indirect(offsets[:]))
+        x_codes = sb.tile([P, D, V], U32, name="x_codes", align_bytes=64)
+        nc.vector.tensor_copy(
+            x_codes[:].rearrange("p d v -> p v d"), word_table[:].bitcast(U32).indirect(offsets[:])
+        )
+        x_scale = sb.tile([P, D, V], U8, name="x_scale", align_bytes=64)
+        nc.vector.tensor_copy(x_scale[:], scale_picked[:].rearrange("p (v d) -> p d v", d=D))
+
+        point_t = []
+        for c in range(2):
+            point_ps = ps.tile([P, 2, N], F32, name="point_ps%d" % c, tag="bank%d" % (6 + c))
+            for h in range(HALVES):
+                nc.tensor.transpose(point_ps[:, 0, h * P : (h + 1) * P], point[c][:, h, :], ident[:])
+            t = sb.tile([P, N], F32, name="point_t%d" % c)
+            nc.scalar.copy(t[:], point_ps[:, 0, :])
+            point_t.append(t)
+
+        disp = []
+        squares = []
+        for c in range(2):
+            grouped = sb.tile([P, N, PACK], BF16, name="grouped%d" % c, align_bytes=64)
+            nc.scalar.copy(
+                grouped[:, :SPLIT, :].rearrange("p (n i) t -> p n t i", i=4),
+                w_raw[c][:, :, :SPLIT].rearrange("p t (n i) -> p n t i", i=4),
+            )
+            nc.gpsimd.tensor_scalar(
+                grouped[:, SPLIT:, :],
+                w_raw[c][:, :, SPLIT:].rearrange("p t n -> p n t"),
+                1.0, 0.0, ALU.mult, ALU.add,
+            )
+            w_codes = sb.tile([P, N], U32, name="w_codes%d" % c, align_bytes=64)
+            w_scale = sb.tile([P, N], U8, name="w_scale%d" % c, align_bytes=64)
+            nc.vector.quantize_mx(
+                out=w_codes[:].bitcast(FP8X4), scales=w_scale[:], in_=grouped[:].rearrange("p n t -> p (n t)")
+            )
+            prods = []
+            if c == 0:
+                for d in range(D):
+                    bank = ps.tile([P, 2, N], F32, name="y%d" % d, tag="bank%d" % d)
+                    prods.append(bank[:, 0, :])
+            else:
+                for d2 in range(2):
+                    bank = ps.tile([P, 2, N], F32, name="z%d" % d2, tag="bank%d" % (4 + d2))
+                    prods.extend([bank[:, 0, :], bank[:, 1, :]])
+            for d in range(D):
+                nc.tensor.matmul_mx(
+                    out=prods[d],
+                    lhsT=x_codes[:, d, :].bitcast(FP8X4),
+                    lhsT_scale=x_scale[:, d, :],
+                    rhs=w_codes[:].bitcast(FP8X4),
+                    rhs_scale=w_scale[:],
+                    start=True,
+                    stop=True,
+                )
+            delta = sb.tile([P, D, N], F32, name="delta%d" % c)
+            sq = sb.tile([P, D, N], F32, name="sq%d" % c)
+            for d in range(D):
+                nc.vector.scalar_tensor_tensor(
+                    delta[:, d, :], prods[d], bond[c][:, d : d + 1], point_t[c][:], ALU.add, ALU.subtract
+                )
+                if d % 2 == 1:
+                    nc.scalar.activation(sq[:, d - 1 : d + 1, :], delta[:, d - 1 : d + 1, :], ACT.Square)
+            disp.append(delta)
+            squares.append(sq)
+
+        len2 = sb.tile([P, D, N], F32, name="len2")
+        rlen = sb.tile([P, D, N], F32, name="rlen")
+        stretch = sb.tile([P, D, N], F32, name="stretch")
+        pull = sb.tile([P, D, N], F32, name="pull")
+        for g in range(2):
+            pair = slice(2 * g, 2 * g + 2)
+            nc.vector.scalar_tensor_tensor(
+                len2[:, pair, :], squares[0][:, pair, :], 0.05, squares[1][:, pair, :], ALU.add, ALU.add
+            )
+            nc.scalar.activation(rlen[:, pair, :], len2[:, pair, :], ACT.Abs_reciprocal_sqrt)
+        warm2 = sb.tile([P, 1], F32, name="warm2")
+        nc.scalar.activation(warm2[:], rlen[:, D - 1, N - 1 : N], ACT.Sigmoid)
+        crit_bias = sb.tile([P, HALVES], F32, name="crit_bias")
+        nc.gpsimd.tensor_scalar(crit_bias[:], crit_col[:, :, 0], -4.0, 0.0, ALU.mult, ALU.add)
+        stretch_t = [ps.tile([P, HALVES, 2, V], F32, name="stretch_t%d" % g, tag="bank%d" % g) for g in range(2)]
+        pull_t = [ps.tile([P, HALVES, 2, V], F32, name="pull_t%d" % g, tag="bank%d" % (2 + g)) for g in range(2)]
+        for d in range(D):
+            nc.vector.scalar_tensor_tensor(
+                stretch[:, d, :], rlen[:, d, :], inv_len[:, d : d + 1], len2[:, d, :], ALU.mult, ALU.mult
+            )
+            for h in range(HALVES):
+                nc.tensor.transpose(stretch_t[d // 2][:, h, d % 2, :], stretch[:, d, h * P : (h + 1) * P], ident[:])
+        for d in range(D):
+            nc.vector.scalar_tensor_tensor(
+                pull[:, d, :], rlen[:, d, :], inv_len[:, d : d + 1], disp[0][:, d, :], ALU.subtract, ALU.mult
+            )
+            for h in range(HALVES):
+                nc.tensor.transpose(pull_t[d // 2][:, h, d % 2, :], pull[:, d, h * P : (h + 1) * P], ident[:])
+
+        force = []
+        for g in range(2):
+            intact = sb.tile([P, HALVES, 2, V], F32, name="intact%d" % g)
+            for h in range(HALVES):
+                nc.scalar.activation(
+                    intact[:, h, :, :], stretch_t[g][:, h, :, :], ACT.Sigmoid, bias=crit_bias[:, h : h + 1], scale=-4.0
+                )
+            t = sb.tile([P, HALVES, 2, V], F32, name="force%d" % g)
+            nc.vector.scalar_tensor_tensor(
+                t[:].rearrange("p h d v -> p (h d v)"), pull_t[g][:].rearrange("p h d v -> p (h d v)"), -1.0,
+                intact[:].rearrange("p h d v -> p (h d v)"), ALU.mult, ALU.mult
+            )
+            force.append(t)
+        first = sb.tile([P, HALVES, V], F32, name="first")
+        nc.gpsimd.tensor_tensor(first[:], force[0][:, :, 0, :], force[0][:, :, 1, :], ALU.add)
+        second = sb.tile([P, HALVES, V], F32, name="second")
+        for h in range(HALVES):
+            nc.vector.tensor_tensor(second[:, h, :], force[1][:, h, 0, :], force[1][:, h, 1, :], ALU.add)
+        for h, queue in enumerate((nc.sync, nc.scalar)):
+            total = sb.tile([P, V], F32, name="total%d" % h)
+            nc.vector.tensor_tensor(total[:], first[:, h, :], second[:, h, :], ALU.add)
+            queue.dma_start(out[h * P : (h + 1) * P, :], total[:])

@@ -7,7 +7,6 @@ K, T, S, D, N, V = 512, 1024, 512, 4, 256, 128
 P = 128
 PACK = 4
 HALVES = N // P
-SPLIT = 144
 FLOPS = 2 * 2 * K * N * S
 
 F32 = mybir.dt.float32
@@ -33,38 +32,32 @@ def tile_picked_yperid_force_p_kernel(
         nc.sync.dma_start(offsets[:], offs)
 
         scale_table = sb.tile([P, T], U8, name="scale_table", align_bytes=64)
-        nc.vector.memset(scale_table[:].bitcast(I32), 0)
         for q in range(4):
-            nc.scalar.dma_start(
-                scale_table[32 * q : 32 * q + 4, :].bitcast(I32),
-                x_scales[0, 4 * q : 4 * q + 4, :].bitcast(I32),
+            (nc.sync if q < 2 else nc.scalar).dma_start(
+                scale_table[32 * q : 32 * q + 32, :].bitcast(I32),
+                x_scales[0, 4 * q : 4 * q + 4, :].bitcast(I32).unsqueeze(0).to_broadcast([8, 4, T // 4]),
             )
         word_table = sb.tile([P, T], I32, name="word_table", align_bytes=64)
         nc.sync.dma_start(word_table[:], x_words[0].rearrange("p n t -> p (n t)").bitcast(I32))
 
-        w_raw = []
-        for c, w in enumerate((w1, w2)):
-            raw = sb.tile([P, PACK, N], F32, name="w_raw%d" % c)
-            nc.sync.dma_start(raw[:], w.rearrange("(p t) n -> p t n", t=PACK))
-            w_raw.append(raw)
+        point = [sb.tile([P, HALVES, V], F32, name="point%d" % c) for c in range(2)]
+        cols = [sb.tile([P, D], F32, name="col%d" % c) for c in range(3)]
+        w_raw = [sb.tile([P, PACK, N], F32, name="w_raw%d" % c) for c in range(2)]
+        nc.scalar.dma_start(point[0][:], px.rearrange("(h p) v -> p h v", p=P))
+        nc.sync.dma_start(w_raw[0][:], w1.rearrange("(p t) n -> p t n", t=PACK))
 
-        ident = sb.tile([P, P], F32, name="ident")
-        make_identity(nc, ident[:])
         one = sb.tile([P, 1], F32, name="one")
         nc.gpsimd.memset(one[:], 1.0)
+        ident = sb.tile([P, P], F32, name="ident")
+        make_identity(nc, ident[:])
         warm = sb.tile([P, 1], F32, name="warm")
         nc.scalar.activation(warm[:], one[:], ACT.Abs_reciprocal_sqrt)
 
-        point = []
-        for c, pt in enumerate((px, py)):
-            t = sb.tile([P, HALVES, V], F32, name="point%d" % c)
-            nc.scalar.dma_start(t[:], pt.rearrange("(h p) v -> p h v", p=P))
-            point.append(t)
-        cols = []
-        for c, row in enumerate((bx, by, il)):
-            t = sb.tile([P, D], F32, name="col%d" % c)
-            nc.sync.dma_start(t[:], row[0:1, :].rearrange("o (v d) -> (o v) d", d=D))
-            cols.append(t)
+        nc.sync.dma_start(w_raw[1][:], w2.rearrange("(p t) n -> p t n", t=PACK))
+        nc.scalar.dma_start(cols[0][:], bx[0:1, :].rearrange("o (v d) -> (o v) d", d=D))
+        nc.scalar.dma_start(point[1][:], py.rearrange("(h p) v -> p h v", p=P))
+        nc.sync.dma_start(cols[1][:], by[0:1, :].rearrange("o (v d) -> (o v) d", d=D))
+        nc.sync.dma_start(cols[2][:], il[0:1, :].rearrange("o (v d) -> (o v) d", d=D))
         bond = cols[:2]
         inv_len = cols[2]
         crit_col = sb.tile([P, HALVES, 1], F32, name="crit_col")
@@ -81,27 +74,23 @@ def tile_picked_yperid_force_p_kernel(
         x_scale = sb.tile([P, D, V], U8, name="x_scale", align_bytes=64)
         nc.vector.tensor_copy(x_scale[:], scale_picked[:].rearrange("p (v d) -> p d v", d=D))
 
-        point_t = []
-        for c in range(2):
+        def turn_points(c):
             point_ps = ps.tile([P, 2, N], F32, name="point_ps%d" % c, tag="bank%d" % (6 + c))
             for h in range(HALVES):
                 nc.tensor.transpose(point_ps[:, 0, h * P : (h + 1) * P], point[c][:, h, :], ident[:])
-            t = sb.tile([P, N], F32, name="point_t%d" % c)
-            nc.scalar.copy(t[:], point_ps[:, 0, :])
-            point_t.append(t)
+            turned = sb.tile([P, N], F32, name="point_t%d" % c)
+            nc.scalar.copy(turned[:], point_ps[:, 0, :])
+            return turned
+
+        point_t = [turn_points(0)]
 
         disp = []
         squares = []
         for c in range(2):
             grouped = sb.tile([P, N, PACK], BF16, name="grouped%d" % c, align_bytes=64)
             nc.scalar.copy(
-                grouped[:, :SPLIT, :].rearrange("p (n i) t -> p n t i", i=4),
-                w_raw[c][:, :, :SPLIT].rearrange("p t (n i) -> p n t i", i=4),
-            )
-            nc.gpsimd.tensor_scalar(
-                grouped[:, SPLIT:, :],
-                w_raw[c][:, :, SPLIT:].rearrange("p t n -> p n t"),
-                1.0, 0.0, ALU.mult, ALU.add,
+                grouped[:].rearrange("p (n i) t -> p n t i", i=4),
+                w_raw[c][:].rearrange("p t (n i) -> p n t i", i=4),
             )
             w_codes = sb.tile([P, N], U32, name="w_codes%d" % c, align_bytes=64)
             w_scale = sb.tile([P, N], U8, name="w_scale%d" % c, align_bytes=64)
@@ -127,13 +116,17 @@ def tile_picked_yperid_force_p_kernel(
                     start=True,
                     stop=True,
                 )
+            if c == 0:
+                point_t.append(turn_points(1))
             delta = sb.tile([P, D, N], F32, name="delta%d" % c)
             sq = sb.tile([P, D, N], F32, name="sq%d" % c)
             for d in range(D):
                 nc.vector.scalar_tensor_tensor(
                     delta[:, d, :], prods[d], bond[c][:, d : d + 1], point_t[c][:], ALU.add, ALU.subtract
                 )
-                if d % 2 == 1:
+                if c == 1 and d >= 2:
+                    nc.scalar.activation(sq[:, d, :], delta[:, d, :], ACT.Square)
+                elif d % 2 == 1:
                     nc.scalar.activation(sq[:, d - 1 : d + 1, :], delta[:, d - 1 : d + 1, :], ACT.Square)
             disp.append(delta)
             squares.append(sq)
@@ -142,8 +135,7 @@ def tile_picked_yperid_force_p_kernel(
         rlen = sb.tile([P, D, N], F32, name="rlen")
         stretch = sb.tile([P, D, N], F32, name="stretch")
         pull = sb.tile([P, D, N], F32, name="pull")
-        for g in range(2):
-            pair = slice(2 * g, 2 * g + 2)
+        for pair in (slice(0, 2), slice(2, 3), slice(3, 4)):
             nc.vector.scalar_tensor_tensor(
                 len2[:, pair, :], squares[0][:, pair, :], 0.05, squares[1][:, pair, :], ALU.add, ALU.add
             )
@@ -154,38 +146,43 @@ def tile_picked_yperid_force_p_kernel(
         nc.gpsimd.tensor_scalar(crit_bias[:], crit_col[:, :, 0], -4.0, 0.0, ALU.mult, ALU.add)
         stretch_t = [ps.tile([P, HALVES, 2, V], F32, name="stretch_t%d" % g, tag="bank%d" % g) for g in range(2)]
         pull_t = [ps.tile([P, HALVES, 2, V], F32, name="pull_t%d" % g, tag="bank%d" % (2 + g)) for g in range(2)]
-        for d in range(D):
-            nc.vector.scalar_tensor_tensor(
-                stretch[:, d, :], rlen[:, d, :], inv_len[:, d : d + 1], len2[:, d, :], ALU.mult, ALU.mult
-            )
-            for h in range(HALVES):
-                nc.tensor.transpose(stretch_t[d // 2][:, h, d % 2, :], stretch[:, d, h * P : (h + 1) * P], ident[:])
-        for d in range(D):
-            nc.vector.scalar_tensor_tensor(
-                pull[:, d, :], rlen[:, d, :], inv_len[:, d : d + 1], disp[0][:, d, :], ALU.subtract, ALU.mult
-            )
-            for h in range(HALVES):
-                nc.tensor.transpose(pull_t[d // 2][:, h, d % 2, :], pull[:, d, h * P : (h + 1) * P], ident[:])
-
-        force = []
         for g in range(2):
-            intact = sb.tile([P, HALVES, 2, V], F32, name="intact%d" % g)
-            for h in range(HALVES):
-                nc.scalar.activation(
-                    intact[:, h, :, :], stretch_t[g][:, h, :, :], ACT.Sigmoid, bias=crit_bias[:, h : h + 1], scale=-4.0
+            for d in (2 * g, 2 * g + 1):
+                nc.vector.scalar_tensor_tensor(
+                    stretch[:, d, :], rlen[:, d, :], inv_len[:, d : d + 1], len2[:, d, :], ALU.mult, ALU.mult
                 )
-            t = sb.tile([P, HALVES, 2, V], F32, name="force%d" % g)
-            nc.vector.scalar_tensor_tensor(
-                t[:].rearrange("p h d v -> p (h d v)"), pull_t[g][:].rearrange("p h d v -> p (h d v)"), -1.0,
-                intact[:].rearrange("p h d v -> p (h d v)"), ALU.mult, ALU.mult
-            )
-            force.append(t)
-        first = sb.tile([P, HALVES, V], F32, name="first")
-        nc.gpsimd.tensor_tensor(first[:], force[0][:, :, 0, :], force[0][:, :, 1, :], ALU.add)
-        second = sb.tile([P, HALVES, V], F32, name="second")
-        for h in range(HALVES):
-            nc.vector.tensor_tensor(second[:, h, :], force[1][:, h, 0, :], force[1][:, h, 1, :], ALU.add)
+                for h in range(HALVES):
+                    nc.tensor.transpose(stretch_t[g][:, h, d % 2, :], stretch[:, d, h * P : (h + 1) * P], ident[:])
+            for d in (2 * g, 2 * g + 1):
+                nc.vector.scalar_tensor_tensor(
+                    pull[:, d, :], rlen[:, d, :], inv_len[:, d : d + 1], disp[0][:, d, :], ALU.subtract, ALU.mult
+                )
+                for h in range(HALVES):
+                    nc.tensor.transpose(pull_t[g][:, h, d % 2, :], pull[:, d, h * P : (h + 1) * P], ident[:])
+
+        parts = [sb.tile([P, 3, V], F32, name="parts%d" % h) for h in range(HALVES)]
+        for g in range(2):
+            for h in range(HALVES):
+                intact = sb.tile([P, 2 * V], F32, name="intact%d%d" % (g, h))
+                nc.scalar.activation(
+                    intact[:], stretch_t[g][:, h, :, :].rearrange("p d v -> p (d v)"), ACT.Sigmoid,
+                    bias=crit_bias[:, h : h + 1], scale=-4.0
+                )
+                if g == 0:
+                    early = sb.tile([P, 2, V], F32, name="early%d" % h)
+                    dst = early[:]
+                else:
+                    dst = parts[h][:, 1:3, :]
+                nc.vector.scalar_tensor_tensor(
+                    dst.rearrange("p d v -> p (d v)"), pull_t[g][:, h, :, :].rearrange("p d v -> p (d v)"), -1.0,
+                    intact[:], ALU.mult, ALU.mult
+                )
+                if g == 0:
+                    nc.gpsimd.tensor_tensor(parts[h][:, 0, :], early[:, 0, :], early[:, 1, :], ALU.add)
+        total = [sb.tile([P, V], F32, name="total%d" % h) for h in range(HALVES)]
+        three = sb.tile([P, V], F32, name="three")
+        nc.gpsimd.tensor_tensor(three[:], parts[0][:, 0, :], parts[0][:, 1, :], ALU.add)
+        nc.gpsimd.tensor_tensor(total[0][:], three[:], parts[0][:, 2, :], ALU.add)
+        nc.vector.tensor_reduce(total[1][:], parts[1][:].rearrange("p d v -> p v d"), mybir.AxisListType.X, ALU.add)
         for h, queue in enumerate((nc.sync, nc.scalar)):
-            total = sb.tile([P, V], F32, name="total%d" % h)
-            nc.vector.tensor_tensor(total[:], first[:, h, :], second[:, h, :], ALU.add)
-            queue.dma_start(out[h * P : (h + 1) * P, :], total[:])
+            queue.dma_start(out[h * P : (h + 1) * P, :], total[h][:])

@@ -40,11 +40,16 @@ def tile_picked_yperid_force_p_kernel(
         word_table = sb.tile([P, T], I32, name="word_table", align_bytes=64)
         nc.sync.dma_start(word_table[:], x_words[0].rearrange("p n t -> p (n t)").bitcast(I32))
 
-        point = [sb.tile([P, HALVES, V], F32, name="point%d" % c) for c in range(2)]
+        point = sb.tile([P, 2, HALVES, V], F32, name="point", tag="w_codes0", align_bytes=64)
         cols = [sb.tile([P, D], F32, name="col%d" % c) for c in range(3)]
-        w_raw = [sb.tile([P, PACK, N], F32, name="w_raw%d" % c) for c in range(2)]
-        nc.scalar.dma_start(point[0][:], px.rearrange("(h p) v -> p h v", p=P))
+        w_raw = [sb.tile([P, PACK, N], F32, name="w_raw%d" % c, tag="w_raw%d" % c) for c in range(2)]
         nc.sync.dma_start(w_raw[0][:], w1.rearrange("(p t) n -> p t n", t=PACK))
+        nc.sync.dma_start(point[:, 0, :, :], px.rearrange("(h p) v -> p h v", p=P))
+        nc.sync.dma_start(point[:, 1, :, :], py.rearrange("(h p) v -> p h v", p=P))
+        nc.sync.dma_start(cols[0][:], bx[0:1, :].rearrange("o (v d) -> (o v) d", d=D))
+        nc.sync.dma_start(w_raw[1][:], w2.rearrange("(p t) n -> p t n", t=PACK))
+        nc.sync.dma_start(cols[1][:], by[0:1, :].rearrange("o (v d) -> (o v) d", d=D))
+        nc.sync.dma_start(cols[2][:], il[0:1, :].rearrange("o (v d) -> (o v) d", d=D))
 
         one = sb.tile([P, 1], F32, name="one")
         nc.gpsimd.memset(one[:], 1.0)
@@ -53,11 +58,6 @@ def tile_picked_yperid_force_p_kernel(
         warm = sb.tile([P, 1], F32, name="warm")
         nc.scalar.activation(warm[:], one[:], ACT.Abs_reciprocal_sqrt)
 
-        nc.sync.dma_start(w_raw[1][:], w2.rearrange("(p t) n -> p t n", t=PACK))
-        nc.scalar.dma_start(cols[0][:], bx[0:1, :].rearrange("o (v d) -> (o v) d", d=D))
-        nc.scalar.dma_start(point[1][:], py.rearrange("(h p) v -> p h v", p=P))
-        nc.sync.dma_start(cols[1][:], by[0:1, :].rearrange("o (v d) -> (o v) d", d=D))
-        nc.sync.dma_start(cols[2][:], il[0:1, :].rearrange("o (v d) -> (o v) d", d=D))
         bond = cols[:2]
         inv_len = cols[2]
         crit_col = sb.tile([P, HALVES, 1], F32, name="crit_col")
@@ -74,41 +74,33 @@ def tile_picked_yperid_force_p_kernel(
         x_scale = sb.tile([P, D, V], U8, name="x_scale", align_bytes=64)
         nc.vector.tensor_copy(x_scale[:], scale_picked[:].rearrange("p (v d) -> p d v", d=D))
 
-        def turn_points(c):
-            point_ps = ps.tile([P, 2, N], F32, name="point_ps%d" % c, tag="bank%d" % (6 + c))
-            for h in range(HALVES):
-                nc.tensor.transpose(point_ps[:, 0, h * P : (h + 1) * P], point[c][:, h, :], ident[:])
-            turned = sb.tile([P, N], F32, name="point_t%d" % c)
-            nc.scalar.copy(turned[:], point_ps[:, 0, :])
-            return turned
-
-        point_t = [turn_points(0)]
-
-        disp = []
-        squares = []
+        point_ps = ps.tile([P, 2, N], F32, name="point_ps", tag="bank6")
         for c in range(2):
-            grouped = sb.tile([P, N, PACK], BF16, name="grouped%d" % c, align_bytes=64)
+            for h in range(HALVES):
+                nc.tensor.transpose(point_ps[:, c, h * P : (h + 1) * P], point[:, c, h, :], ident[:])
+        point_t = sb.tile([P, 2, N], F32, name="point_t")
+
+        def round_weights(c):
+            grouped = sb.tile([P, N, PACK], BF16, name="grouped%d" % c, tag="grouped%d" % c, align_bytes=64)
             nc.scalar.copy(
                 grouped[:].rearrange("p (n i) t -> p n t i", i=4),
                 w_raw[c][:].rearrange("p t (n i) -> p n t i", i=4),
             )
-            w_codes = sb.tile([P, N], U32, name="w_codes%d" % c, align_bytes=64)
+            return grouped
+
+        def quantise(c, grouped):
+            w_codes = sb.tile([P, N], U32, name="w_codes%d" % c, tag="w_codes%d" % c, align_bytes=64)
             w_scale = sb.tile([P, N], U8, name="w_scale%d" % c, align_bytes=64)
             nc.vector.quantize_mx(
                 out=w_codes[:].bitcast(FP8X4), scales=w_scale[:], in_=grouped[:].rearrange("p n t -> p (n t)")
             )
-            prods = []
-            if c == 0:
-                for d in range(D):
-                    bank = ps.tile([P, 2, N], F32, name="y%d" % d, tag="bank%d" % d)
-                    prods.append(bank[:, 0, :])
-            else:
-                for d2 in range(2):
-                    bank = ps.tile([P, 2, N], F32, name="z%d" % d2, tag="bank%d" % (4 + d2))
-                    prods.extend([bank[:, 0, :], bank[:, 1, :]])
+            return w_codes, w_scale
+
+        def products(quantised, targets):
+            w_codes, w_scale = quantised
             for d in range(D):
                 nc.tensor.matmul_mx(
-                    out=prods[d],
+                    out=targets[d],
                     lhsT=x_codes[:, d, :].bitcast(FP8X4),
                     lhsT_scale=x_scale[:, d, :],
                     rhs=w_codes[:].bitcast(FP8X4),
@@ -116,73 +108,82 @@ def tile_picked_yperid_force_p_kernel(
                     start=True,
                     stop=True,
                 )
-            if c == 0:
-                point_t.append(turn_points(1))
-            delta = sb.tile([P, D, N], F32, name="delta%d" % c)
-            sq = sb.tile([P, D, N], F32, name="sq%d" % c)
-            for d in range(D):
-                nc.vector.scalar_tensor_tensor(
-                    delta[:, d, :], prods[d], bond[c][:, d : d + 1], point_t[c][:], ALU.add, ALU.subtract
-                )
-                if c == 1 and d >= 2:
-                    nc.scalar.activation(sq[:, d, :], delta[:, d, :], ACT.Square)
-                elif d % 2 == 1:
-                    nc.scalar.activation(sq[:, d - 1 : d + 1, :], delta[:, d - 1 : d + 1, :], ACT.Square)
-            disp.append(delta)
-            squares.append(sq)
+
+        def displace(c, d, product, delta):
+            nc.vector.scalar_tensor_tensor(
+                delta, product, bond[c][:, d : d + 1], point_t[:, c, :], ALU.add, ALU.subtract
+            )
+
+        squares = [sb.tile([P, D, N], F32, name="sq%d" % c) for c in range(2)]
+        grouped = [round_weights(c) for c in range(2)]
+        first = quantise(0, grouped[0])
+        nc.vector.tensor_copy(point_t[:], point_ps[:])
+        y_banks = [ps.tile([P, 2, N], F32, name="y%d" % d, tag="bank%d" % d) for d in range(D)]
+        y = [bank[:, 0, :] for bank in y_banks]
+        products(first, y)
+        dx_early = sb.tile([P, 2, N], F32, name="dx_early")
+        for d in range(2):
+            displace(0, d, y[d], dx_early[:, d, :])
+        nc.scalar.activation(squares[0][:, 0:2, :], dx_early[:], ACT.Square)
+        second = quantise(1, grouped[1])
+        z_banks = [ps.tile([P, 2, N], F32, name="z%d" % g, tag="bank%d" % b) for g, b in enumerate((4, 5, 7))]
+        z = [z_banks[0][:, 0, :], z_banks[1][:, 0, :], z_banks[2][:, 0, :], z_banks[2][:, 1, :]]
+        products(second, z)
+        dx_late = sb.tile([P, 2, N], F32, name="dx_late", tag="grouped1", align_bytes=64)
+        for d in range(2):
+            displace(0, 2 + d, y[2 + d], dx_late[:, d, :])
+        nc.scalar.activation(squares[0][:, 2:4, :], dx_late[:], ACT.Square)
+        dx = [dx_early[:, 0, :], dx_early[:, 1, :], dx_late[:, 0, :], dx_late[:, 1, :]]
+        dy = sb.tile([P, D, N], F32, name="dy")
+        for d in range(D):
+            displace(1, d, z[d], dy[:, d, :])
+            nc.scalar.activation(squares[1][:, d, :], dy[:, d, :], ACT.Square)
 
         len2 = sb.tile([P, D, N], F32, name="len2")
         rlen = sb.tile([P, D, N], F32, name="rlen")
         stretch = sb.tile([P, D, N], F32, name="stretch")
         pull = sb.tile([P, D, N], F32, name="pull")
-        for pair in (slice(0, 2), slice(2, 3), slice(3, 4)):
+        for pair in range(D):
             nc.vector.scalar_tensor_tensor(
                 len2[:, pair, :], squares[0][:, pair, :], 0.05, squares[1][:, pair, :], ALU.add, ALU.add
             )
             nc.scalar.activation(rlen[:, pair, :], len2[:, pair, :], ACT.Abs_reciprocal_sqrt)
         warm2 = sb.tile([P, 1], F32, name="warm2")
         nc.scalar.activation(warm2[:], rlen[:, D - 1, N - 1 : N], ACT.Sigmoid)
-        crit_bias = sb.tile([P, HALVES], F32, name="crit_bias")
+        crit_bias = sb.tile([P, HALVES], F32, name="crit_bias", tag="w_raw1")
         nc.gpsimd.tensor_scalar(crit_bias[:], crit_col[:, :, 0], -4.0, 0.0, ALU.mult, ALU.add)
-        stretch_t = [ps.tile([P, HALVES, 2, V], F32, name="stretch_t%d" % g, tag="bank%d" % g) for g in range(2)]
-        pull_t = [ps.tile([P, HALVES, 2, V], F32, name="pull_t%d" % g, tag="bank%d" % (2 + g)) for g in range(2)]
-        for g in range(2):
-            for d in (2 * g, 2 * g + 1):
-                nc.vector.scalar_tensor_tensor(
-                    stretch[:, d, :], rlen[:, d, :], inv_len[:, d : d + 1], len2[:, d, :], ALU.mult, ALU.mult
-                )
-                for h in range(HALVES):
-                    nc.tensor.transpose(stretch_t[g][:, h, d % 2, :], stretch[:, d, h * P : (h + 1) * P], ident[:])
-            for d in (2 * g, 2 * g + 1):
-                nc.vector.scalar_tensor_tensor(
-                    pull[:, d, :], rlen[:, d, :], inv_len[:, d : d + 1], disp[0][:, d, :], ALU.subtract, ALU.mult
-                )
-                for h in range(HALVES):
-                    nc.tensor.transpose(pull_t[g][:, h, d % 2, :], pull[:, d, h * P : (h + 1) * P], ident[:])
-
-        parts = [sb.tile([P, 3, V], F32, name="parts%d" % h) for h in range(HALVES)]
-        for g in range(2):
+        stretch_t = [ps.tile([P, D, V], F32, name="stretch_t%d" % h, tag="bank%d" % h) for h in range(HALVES)]
+        pull_t = [ps.tile([P, D, V], F32, name="pull_t%d" % h, tag="bank%d" % (2 + h)) for h in range(HALVES)]
+        for d in range(D):
+            nc.vector.scalar_tensor_tensor(
+                stretch[:, d, :], rlen[:, d, :], inv_len[:, d : d + 1], len2[:, d, :], ALU.mult, ALU.mult
+            )
             for h in range(HALVES):
-                intact = sb.tile([P, 2 * V], F32, name="intact%d%d" % (g, h))
-                nc.scalar.activation(
-                    intact[:], stretch_t[g][:, h, :, :].rearrange("p d v -> p (d v)"), ACT.Sigmoid,
-                    bias=crit_bias[:, h : h + 1], scale=-4.0
-                )
-                if g == 0:
-                    early = sb.tile([P, 2, V], F32, name="early%d" % h)
-                    dst = early[:]
-                else:
-                    dst = parts[h][:, 1:3, :]
+                nc.tensor.transpose(stretch_t[h][:, d, :], stretch[:, d, h * P : (h + 1) * P], ident[:])
+        for h in range(HALVES):
+            rows = slice(h * P, (h + 1) * P)
+            for d in range(D):
                 nc.vector.scalar_tensor_tensor(
-                    dst.rearrange("p d v -> p (d v)"), pull_t[g][:, h, :, :].rearrange("p d v -> p (d v)"), -1.0,
-                    intact[:], ALU.mult, ALU.mult
+                    pull[:, d, rows], rlen[:, d, rows], inv_len[:, d : d + 1], dx[d][:, rows], ALU.subtract, ALU.mult
                 )
-                if g == 0:
-                    nc.gpsimd.tensor_tensor(parts[h][:, 0, :], early[:, 0, :], early[:, 1, :], ALU.add)
+                nc.tensor.transpose(pull_t[h][:, d, :], pull[:, d, rows], ident[:])
+
+        force = [sb.tile([P, D, V], F32, name="force%d" % h) for h in range(HALVES)]
+        for h in range(HALVES):
+            intact = sb.tile([P, D * V], F32, name="intact%d" % h)
+            nc.scalar.activation(
+                intact[:], stretch_t[h][:].rearrange("p d v -> p (d v)"), ACT.Sigmoid,
+                bias=crit_bias[:, h : h + 1], scale=-4.0
+            )
+            nc.vector.scalar_tensor_tensor(
+                force[h][:].rearrange("p d v -> p (d v)"),
+                pull_t[h][:].rearrange("p d v -> p (d v)"), -1.0,
+                intact[:], ALU.mult, ALU.mult
+            )
         total = [sb.tile([P, V], F32, name="total%d" % h) for h in range(HALVES)]
-        three = sb.tile([P, V], F32, name="three")
-        nc.gpsimd.tensor_tensor(three[:], parts[0][:, 0, :], parts[0][:, 1, :], ALU.add)
-        nc.gpsimd.tensor_tensor(total[0][:], three[:], parts[0][:, 2, :], ALU.add)
-        nc.vector.tensor_reduce(total[1][:], parts[1][:].rearrange("p d v -> p v d"), mybir.AxisListType.X, ALU.add)
+        pairs = sb.tile([P, 2, V], F32, name="pairs")
+        nc.gpsimd.tensor_tensor(pairs[:], force[0][:, 0:2, :], force[0][:, 2:4, :], ALU.add)
+        nc.gpsimd.tensor_tensor(total[0][:], pairs[:, 0, :], pairs[:, 1, :], ALU.add)
+        nc.vector.tensor_reduce(total[1][:], force[1][:].rearrange("p d v -> p v d"), mybir.AxisListType.X, ALU.add)
         for h, queue in enumerate((nc.sync, nc.scalar)):
             queue.dma_start(out[h * P : (h + 1) * P, :], total[h][:])

@@ -7,6 +7,7 @@ K, T, S, D, N, V = 512, 1024, 512, 4, 256, 128
 P = 128
 PACK = 4
 HALVES = N // P
+SCALAR_COLUMNS = (192, 160)
 FLOPS = 2 * 2 * K * N * S
 
 F32 = mybir.dt.float32
@@ -40,14 +41,17 @@ def tile_picked_yperid_force_p_kernel(
         word_table = sb.tile([P, T], I32, name="word_table", align_bytes=64)
         nc.sync.dma_start(word_table[:], x_words[0].rearrange("p n t -> p (n t)").bitcast(I32))
 
-        point = sb.tile([P, 2, HALVES, V], F32, name="point", tag="w_codes0", align_bytes=64)
+        point = [
+            sb.tile([P, HALVES, V], F32, name="point%d" % c, tag=("w_codes0", "point1")[c], align_bytes=64)
+            for c in range(2)
+        ]
         cols = [sb.tile([P, D], F32, name="col%d" % c) for c in range(3)]
         w_raw = [sb.tile([P, PACK, N], F32, name="w_raw%d" % c, tag="w_raw%d" % c) for c in range(2)]
         nc.sync.dma_start(w_raw[0][:], w1.rearrange("(p t) n -> p t n", t=PACK))
-        nc.sync.dma_start(point[:, 0, :, :], px.rearrange("(h p) v -> p h v", p=P))
-        nc.sync.dma_start(point[:, 1, :, :], py.rearrange("(h p) v -> p h v", p=P))
-        nc.sync.dma_start(cols[0][:], bx[0:1, :].rearrange("o (v d) -> (o v) d", d=D))
+        nc.sync.dma_start(point[0][:], px.rearrange("(h p) v -> p h v", p=P))
+        nc.sync.dma_start(point[1][:], py.rearrange("(h p) v -> p h v", p=P))
         nc.sync.dma_start(w_raw[1][:], w2.rearrange("(p t) n -> p t n", t=PACK))
+        nc.sync.dma_start(cols[0][:], bx[0:1, :].rearrange("o (v d) -> (o v) d", d=D))
         nc.sync.dma_start(cols[1][:], by[0:1, :].rearrange("o (v d) -> (o v) d", d=D))
         nc.sync.dma_start(cols[2][:], il[0:1, :].rearrange("o (v d) -> (o v) d", d=D))
 
@@ -74,18 +78,31 @@ def tile_picked_yperid_force_p_kernel(
         x_scale = sb.tile([P, D, V], U8, name="x_scale", align_bytes=64)
         nc.vector.tensor_copy(x_scale[:], scale_picked[:].rearrange("p (v d) -> p d v", d=D))
 
-        point_ps = ps.tile([P, 2, N], F32, name="point_ps", tag="bank6")
+        y_banks = [ps.tile([P, 2, N], F32, name="y%d" % d, tag="bank%d" % d) for d in range(D)]
+        px_bank = ps.tile([P, 2, N], F32, name="px_bank", tag="bank6")
+        point_ps = [px_bank[:, 0, :], y_banks[0][:, 1, :]]
         for c in range(2):
             for h in range(HALVES):
-                nc.tensor.transpose(point_ps[:, c, h * P : (h + 1) * P], point[:, c, h, :], ident[:])
-        point_t = sb.tile([P, 2, N], F32, name="point_t")
+                nc.tensor.transpose(point_ps[c][:, h * P : (h + 1) * P], point[c][:, h, :], ident[:])
+        point_t = [sb.tile([P, N], F32, name="point_t%d" % c) for c in range(2)]
 
         def round_weights(c):
-            grouped = sb.tile([P, N, PACK], BF16, name="grouped%d" % c, tag="grouped%d" % c, align_bytes=64)
+            grouped = sb.tile([P, N, PACK], BF16, name="grouped%d" % c, tag="grouped", align_bytes=64)
+            split = SCALAR_COLUMNS[c]
             nc.scalar.copy(
-                grouped[:].rearrange("p (n i) t -> p n t i", i=4),
-                w_raw[c][:].rearrange("p t (n i) -> p n t i", i=4),
+                grouped[:, :split, :].rearrange("p (n i) t -> p n t i", i=4),
+                w_raw[c][:, :, :split].rearrange("p t (n i) -> p n t i", i=4),
             )
+            if c == 0:
+                nc.vector.tensor_copy(
+                    grouped[:, split:, :].rearrange("p (n i) t -> p n t i", i=4),
+                    w_raw[c][:, :, split:].rearrange("p t (n i) -> p n t i", i=4),
+                )
+            else:
+                nc.gpsimd.tensor_scalar(
+                    grouped[:, split:, :], w_raw[c][:, :, split:].rearrange("p t n -> p n t"),
+                    1.0, 0.0, ALU.mult, ALU.add,
+                )
             return grouped
 
         def quantise(c, grouped):
@@ -111,25 +128,25 @@ def tile_picked_yperid_force_p_kernel(
 
         def displace(c, d, product, delta):
             nc.vector.scalar_tensor_tensor(
-                delta, product, bond[c][:, d : d + 1], point_t[:, c, :], ALU.add, ALU.subtract
+                delta, product, bond[c][:, d : d + 1], point_t[c][:], ALU.add, ALU.subtract
             )
 
         squares = [sb.tile([P, D, N], F32, name="sq%d" % c) for c in range(2)]
-        grouped = [round_weights(c) for c in range(2)]
-        first = quantise(0, grouped[0])
-        nc.vector.tensor_copy(point_t[:], point_ps[:])
-        y_banks = [ps.tile([P, 2, N], F32, name="y%d" % d, tag="bank%d" % d) for d in range(D)]
+        first = quantise(0, round_weights(0))
+        nc.vector.tensor_copy(point_t[0][:], point_ps[0])
+        second_rounded = round_weights(1)
         y = [bank[:, 0, :] for bank in y_banks]
         products(first, y)
         dx_early = sb.tile([P, 2, N], F32, name="dx_early")
         for d in range(2):
             displace(0, d, y[d], dx_early[:, d, :])
+        nc.scalar.copy(point_t[1][:], point_ps[1])
         nc.scalar.activation(squares[0][:, 0:2, :], dx_early[:], ACT.Square)
-        second = quantise(1, grouped[1])
+        second = quantise(1, second_rounded)
         z_banks = [ps.tile([P, 2, N], F32, name="z%d" % g, tag="bank%d" % b) for g, b in enumerate((4, 5, 7))]
         z = [z_banks[0][:, 0, :], z_banks[1][:, 0, :], z_banks[2][:, 0, :], z_banks[2][:, 1, :]]
         products(second, z)
-        dx_late = sb.tile([P, 2, N], F32, name="dx_late", tag="grouped1", align_bytes=64)
+        dx_late = sb.tile([P, 2, N], F32, name="dx_late", tag="grouped", align_bytes=64)
         for d in range(2):
             displace(0, 2 + d, y[2 + d], dx_late[:, d, :])
         nc.scalar.activation(squares[0][:, 2:4, :], dx_late[:], ACT.Square)
@@ -170,16 +187,15 @@ def tile_picked_yperid_force_p_kernel(
 
         force = [sb.tile([P, D, V], F32, name="force%d" % h) for h in range(HALVES)]
         for h in range(HALVES):
-            intact = sb.tile([P, D * V], F32, name="intact%d" % h)
-            nc.scalar.activation(
-                intact[:], stretch_t[h][:].rearrange("p d v -> p (d v)"), ACT.Sigmoid,
-                bias=crit_bias[:, h : h + 1], scale=-4.0
-            )
-            nc.vector.scalar_tensor_tensor(
-                force[h][:].rearrange("p d v -> p (d v)"),
-                pull_t[h][:].rearrange("p d v -> p (d v)"), -1.0,
-                intact[:], ALU.mult, ALU.mult
-            )
+            intact = sb.tile([P, D, V], F32, name="intact%d" % h)
+            for pair in (slice(0, 2), slice(2, 4)):
+                nc.scalar.activation(
+                    intact[:, pair, :], stretch_t[h][:, pair, :], ACT.Sigmoid,
+                    bias=crit_bias[:, h : h + 1], scale=-4.0
+                )
+                nc.vector.scalar_tensor_tensor(
+                    force[h][:, pair, :], pull_t[h][:, pair, :], -1.0, intact[:, pair, :], ALU.mult, ALU.mult
+                )
         total = [sb.tile([P, V], F32, name="total%d" % h) for h in range(HALVES)]
         pairs = sb.tile([P, 2, V], F32, name="pairs")
         nc.gpsimd.tensor_tensor(pairs[:], force[0][:, 0:2, :], force[0][:, 2:4, :], ALU.add)

from contextlib import ExitStack

import concourse.mybir as mybir
from concourse.masks import make_identity

K, T, S, D, N, V = 512, 1024, 512, 4, 256, 128
P = 128
PACK = 4
HALVES = N // P
SCALAR_COLUMNS = (192, 160)
FLOPS = 2 * 2 * K * N * S

F32 = mybir.dt.float32
BF16 = mybir.dt.bfloat16
I32 = mybir.dt.int32
U32 = mybir.dt.uint32
U16 = mybir.dt.uint16
U8 = mybir.dt.uint8
FP8X4 = mybir.dt.float8_e4m3fn_x4
ALU = mybir.AluOpType
ACT = mybir.ActivationFunctionType


def tile_picked_yperid_force_p_kernel(
    tc, x_words, x_scales, w1, w2, px, py, bx, by, il, crit, offs, out
):
    nc = tc.nc
    with ExitStack() as ctx:
        sb = ctx.enter_context(tc.tile_pool(name="sb", bufs=1))
        ps = ctx.enter_context(tc.psum_pool(name="ps", bufs=1))

        offsets = sb.tile([P, S // 16], U16, name="offsets")
        nc.sync.dma_start(offsets[:], offs)

        scale_table = sb.tile([P, T], U8, name="scale_table", align_bytes=64)
        for q in range(4):
            (nc.sync if q < 2 else nc.scalar).dma_start(
                scale_table[32 * q : 32 * q + 32, :].bitcast(I32),
                x_scales[0, 4 * q : 4 * q + 4, :].bitcast(I32).unsqueeze(0).to_broadcast([8, 4, T // 4]),
            )
        word_table = sb.tile([P, T], I32, name="word_table", align_bytes=64)
        nc.sync.dma_start(word_table[:], x_words[0].rearrange("p n t -> p (n t)").bitcast(I32))

        point = [
            sb.tile([P, HALVES, V], F32, name="point%d" % c, tag=("w_codes0", "point1")[c], align_bytes=64)
            for c in range(2)
        ]
        cols = [sb.tile([P, D], F32, name="col%d" % c) for c in range(3)]
        w_raw = [sb.tile([P, PACK, N], F32, name="w_raw%d" % c, tag="w_raw%d" % c) for c in range(2)]
        nc.sync.dma_start(w_raw[0][:], w1.rearrange("(p t) n -> p t n", t=PACK))
        nc.sync.dma_start(point[0][:], px.rearrange("(h p) v -> p h v", p=P))
        nc.sync.dma_start(point[1][:], py.rearrange("(h p) v -> p h v", p=P))
        nc.sync.dma_start(w_raw[1][:], w2.rearrange("(p t) n -> p t n", t=PACK))
        nc.sync.dma_start(cols[0][:], bx[0:1, :].rearrange("o (v d) -> (o v) d", d=D))
        nc.sync.dma_start(cols[1][:], by[0:1, :].rearrange("o (v d) -> (o v) d", d=D))
        nc.sync.dma_start(cols[2][:], il[0:1, :].rearrange("o (v d) -> (o v) d", d=D))

        one = sb.tile([P, 1], F32, name="one")
        nc.gpsimd.memset(one[:], 1.0)
        ident = sb.tile([P, P], F32, name="ident")
        make_identity(nc, ident[:])
        warm = sb.tile([P, 1], F32, name="warm")
        nc.scalar.activation(warm[:], one[:], ACT.Abs_reciprocal_sqrt)

        bond = cols[:2]
        inv_len = cols[2]
        crit_col = sb.tile([P, HALVES, 1], F32, name="crit_col")
        with nc.allow_non_contiguous_dma(reason="one value a partition"):
            nc.sync.dma_start(crit_col[:], crit.rearrange("(h p) o -> p h o", p=P))


        scale_picked = sb.tile([P, S], U8, name="scale_picked", align_bytes=64)
        nc.vector.tensor_copy(scale_picked[:], scale_table[:].indirect(offsets[:]))
        x_codes = sb.tile([P, D, V], U32, name="x_codes", align_bytes=64)
        nc.vector.tensor_copy(
            x_codes[:].rearrange("p d v -> p v d"), word_table[:].bitcast(U32).indirect(offsets[:])
        )
        x_scale = sb.tile([P, D, V], U8, name="x_scale", align_bytes=64)
        nc.vector.tensor_copy(x_scale[:], scale_picked[:].rearrange("p (v d) -> p d v", d=D))

        y_banks = [ps.tile([P, 2, N], F32, name="y%d" % d, tag="bank%d" % d) for d in range(D)]
        px_bank = ps.tile([P, 2, N], F32, name="px_bank", tag="bank6")
        point_ps = [px_bank[:, 0, :], y_banks[0][:, 1, :]]
        for c in range(2):
            for h in range(HALVES):
                nc.tensor.transpose(point_ps[c][:, h * P : (h + 1) * P], point[c][:, h, :], ident[:])
        point_t = [sb.tile([P, N], F32, name="point_t%d" % c) for c in range(2)]

        def round_weights(c):
            grouped = sb.tile([P, N, PACK], BF16, name="grouped%d" % c, tag="grouped", align_bytes=64)
            split = SCALAR_COLUMNS[c]
            nc.scalar.copy(
                grouped[:, :split, :].rearrange("p (n i) t -> p n t i", i=4),
                w_raw[c][:, :, :split].rearrange("p t (n i) -> p n t i", i=4),
            )
            if c == 0:
                nc.vector.tensor_copy(
                    grouped[:, split:, :].rearrange("p (n i) t -> p n t i", i=4),
                    w_raw[c][:, :, split:].rearrange("p t (n i) -> p n t i", i=4),
                )
            else:
                nc.gpsimd.tensor_scalar(
                    grouped[:, split:, :], w_raw[c][:, :, split:].rearrange("p t n -> p n t"),
                    1.0, 0.0, ALU.mult, ALU.add,
                )
            return grouped

        def quantise(c, grouped):
            w_codes = sb.tile([P, N], U32, name="w_codes%d" % c, tag="w_codes%d" % c, align_bytes=64)
            w_scale = sb.tile([P, N], U8, name="w_scale%d" % c, align_bytes=64)
            nc.vector.quantize_mx(
                out=w_codes[:].bitcast(FP8X4), scales=w_scale[:], in_=grouped[:].rearrange("p n t -> p (n t)")
            )
            return w_codes, w_scale

        def products(quantised, targets):
            w_codes, w_scale = quantised
            for d in range(D):
                nc.tensor.matmul_mx(
                    out=targets[d],
                    lhsT=x_codes[:, d, :].bitcast(FP8X4),
                    lhsT_scale=x_scale[:, d, :],
                    rhs=w_codes[:].bitcast(FP8X4),
                    rhs_scale=w_scale[:],
                    start=True,
                    stop=True,
                )

        def displace(c, d, product, delta):
            nc.vector.scalar_tensor_tensor(
                delta, product, bond[c][:, d : d + 1], point_t[c][:], ALU.add, ALU.subtract
            )

        squares = [sb.tile([P, D, N], F32, name="sq%d" % c) for c in range(2)]
        first = quantise(0, round_weights(0))
        nc.vector.tensor_copy(point_t[0][:], point_ps[0])
        second_rounded = round_weights(1)
        y = [bank[:, 0, :] for bank in y_banks]
        products(first, y)
        dx_early = sb.tile([P, 2, N], F32, name="dx_early")
        for d in range(2):
            displace(0, d, y[d], dx_early[:, d, :])
        nc.scalar.copy(point_t[1][:], point_ps[1])
        nc.scalar.activation(squares[0][:, 0:2, :], dx_early[:], ACT.Square)
        second = quantise(1, second_rounded)
        z_banks = [ps.tile([P, 2, N], F32, name="z%d" % g, tag="bank%d" % b) for g, b in enumerate((4, 5, 7))]
        z = [z_banks[0][:, 0, :], z_banks[1][:, 0, :], z_banks[2][:, 0, :], z_banks[2][:, 1, :]]
        products(second, z)
        dx_late = sb.tile([P, 2, N], F32, name="dx_late", tag="grouped", align_bytes=64)
        for d in range(2):
            displace(0, 2 + d, y[2 + d], dx_late[:, d, :])
        nc.scalar.activation(squares[0][:, 2:4, :], dx_late[:], ACT.Square)
        dx = [dx_early[:, 0, :], dx_early[:, 1, :], dx_late[:, 0, :], dx_late[:, 1, :]]
        dy = sb.tile([P, D, N], F32, name="dy")
        for d in range(D):
            displace(1, d, z[d], dy[:, d, :])
            nc.scalar.activation(squares[1][:, d, :], dy[:, d, :], ACT.Square)

        len2 = sb.tile([P, D, N], F32, name="len2")
        rlen = sb.tile([P, D, N], F32, name="rlen")
        stretch = sb.tile([P, D, N], F32, name="stretch")
        pull = sb.tile([P, D, N], F32, name="pull")
        for pair in range(D):
            nc.vector.scalar_tensor_tensor(
                len2[:, pair, :], squares[0][:, pair, :], 0.05, squares[1][:, pair, :], ALU.add, ALU.add
            )
            nc.scalar.activation(rlen[:, pair, :], len2[:, pair, :], ACT.Abs_reciprocal_sqrt)
        warm2 = sb.tile([P, 1], F32, name="warm2")
        nc.scalar.activation(warm2[:], rlen[:, D - 1, N - 1 : N], ACT.Sigmoid)
        crit_bias = sb.tile([P, HALVES], F32, name="crit_bias", tag="w_raw1")
        nc.gpsimd.tensor_scalar(crit_bias[:], crit_col[:, :, 0], -4.0, 0.0, ALU.mult, ALU.add)
        stretch_t = [ps.tile([P, D, V], F32, name="stretch_t%d" % h, tag="bank%d" % h) for h in range(HALVES)]
        pull_t = [ps.tile([P, D, V], F32, name="pull_t%d" % h, tag="bank%d" % (2 + h)) for h in range(HALVES)]
        for d in range(D):
            nc.vector.scalar_tensor_tensor(
                stretch[:, d, :], rlen[:, d, :], inv_len[:, d : d + 1], len2[:, d, :], ALU.mult, ALU.mult
            )
            for h in range(HALVES):
                nc.tensor.transpose(stretch_t[h][:, d, :], stretch[:, d, h * P : (h + 1) * P], ident[:])
        for h in range(HALVES):
            rows = slice(h * P, (h + 1) * P)
            for d in range(D):
                nc.vector.scalar_tensor_tensor(
                    pull[:, d, rows], rlen[:, d, rows], inv_len[:, d : d + 1], dx[d][:, rows], ALU.subtract, ALU.mult
                )
                nc.tensor.transpose(pull_t[h][:, d, :], pull[:, d, rows], ident[:])

        force = [sb.tile([P, D, V], F32, name="force%d" % h) for h in range(HALVES)]
        for h in range(HALVES):
            intact = sb.tile([P, D, V], F32, name="intact%d" % h)
            for pair in (slice(0, 2), slice(2, 4)):
                nc.scalar.activation(
                    intact[:, pair, :], stretch_t[h][:, pair, :], ACT.Sigmoid,
                    bias=crit_bias[:, h : h + 1], scale=-4.0
                )
                nc.vector.scalar_tensor_tensor(
                    force[h][:, pair, :], pull_t[h][:, pair, :], -1.0, intact[:, pair, :], ALU.mult, ALU.mult
                )
        total = [sb.tile([P, V], F32, name="total%d" % h) for h in range(HALVES)]
        pairs = sb.tile([P, 2, V], F32, name="pairs")
        nc.gpsimd.tensor_tensor(pairs[:], force[0][:, 0:2, :], force[0][:, 2:4, :], ALU.add)
        nc.gpsimd.tensor_tensor(total[0][:], pairs[:, 0, :], pairs[:, 1, :], ALU.add)
        nc.vector.tensor_reduce(total[1][:], force[1][:].rearrange("p d v -> p v d"), mybir.AxisListType.X, ALU.add)
        for h, queue in enumerate((nc.sync, nc.scalar)):
            queue.dma_start(out[h * P : (h + 1) * P, :], total[h][:])
